import numpy as np
import ml_dtypes


def mxq(x, axis, fmt="e4m3"):
    dtype, down = {"e4m3": (ml_dtypes.float8_e4m3fn, 7), "e5m2": (ml_dtypes.float8_e5m2, 14)}[fmt]
    v = np.moveaxis(np.asarray(x, np.float32).astype(ml_dtypes.bfloat16).astype(np.float64), axis, -1)
    blocks = v.reshape(v.shape[:-1] + (-1, 32))
    amax = np.abs(blocks).max(-1, keepdims=True)
    byte = np.maximum(np.where(amax > 0, np.frexp(amax)[1] - 1 + 127, 0) - down, 1)
    scale = np.exp2(byte - 127.0)
    codes = (blocks / scale).astype(np.float32).astype(dtype).astype(np.float64)
    return np.moveaxis((codes * scale).reshape(v.shape), -1, axis)


WIDE = False


def mx_kscale(k):
    if not WIDE:
        return np.ones(k)
    levels = np.array([10, -10, 5, -5, 0])
    if k % 512:
        return np.exp2(np.random.permutation(np.resize(levels, k // 32))).repeat(32)
    a = np.empty((k // 512, 16))
    for p in range(k // 512):
        a[p, :8] = np.random.permutation(np.resize(levels, 8))
        for g in range(8):
            far = levels[np.abs(levels - a[p, g]) >= 10]
            a[p, g + 8] = far[np.random.randint(len(far))]
    return np.exp2(a.ravel()).repeat(32)


def f64(x):
    return np.asarray(x).astype(np.float64)


def striped(idx):
    return np.tile(idx.reshape(-1, 16).T, (8, 1)).astype(np.uint16)


def unstriped(offs):
    return offs[:16].T.reshape(-1).astype(np.int64)


def striped8(idx):
    return np.concatenate([x.reshape(-1, 16).T for x in idx]).astype(np.uint16)


def runs(offs, k):
    lists = np.stack([offs[16 * r : 16 * r + 16].T.reshape(-1) for r in range(8)]).astype(np.int64)
    return lists[np.arange(k) % 512 // 64]


def pack_weight(w):
    k, n = w.shape
    w = f64(np.asarray(w, np.float32).astype(ml_dtypes.bfloat16)).reshape(k // 32, 32, n)
    amax = np.abs(w).max(1)
    byte = np.clip(np.where(amax > 0, np.frexp(amax)[1] - 1 + 127 - 7, 1), 1, 254)
    scaled = (w * np.exp2(127.0 - byte)[:, None, :]).reshape(k, n).astype(np.float32)
    words = np.ascontiguousarray(scaled.reshape(k // 512, 128, 4, n).transpose(0, 1, 3, 2)).astype(ml_dtypes.float8_e4m3fn).view(np.uint8)
    return words, np.ascontiguousarray(byte.astype(np.uint8).reshape(k // 512, 16, n))


def unpack_weight(words, scales):
    g, p, n, _ = words.shape
    vals = np.ascontiguousarray(words).view(ml_dtypes.float8_e4m3fn).astype(np.float64) * np.repeat(np.exp2(scales.astype(np.float64) - 127.0), 8, axis=1)[..., None]
    return vals.transpose(0, 1, 3, 2).reshape(g * 512, n)


def relu(v):
    return np.maximum(v, 0.0)

def planes(y):
    n, m = y.shape
    v = y.astype(np.float32).astype(ml_dtypes.bfloat16).astype(np.float64).reshape(n // 32, 32, m)
    top = np.abs(v).max(1)
    byte = np.clip(np.where(top > 0, np.frexp(top)[1] - 1 + 127 - 7, 1), 1, 254)
    codes = (v * np.exp2(127.0 - byte)[:, None, :]).reshape(n, m).astype(np.float32).astype(ml_dtypes.float8_e4m3fn).view(np.uint8)
    words = codes.reshape(n // 512, 128, 4, m).transpose(0, 1, 3, 2)
    return np.ascontiguousarray(words), np.ascontiguousarray(byte.astype(np.uint8).reshape(n // 512, 16, m))


K, T, S, N, H = 512, 2048, 512, 512, 512


def setup_inputs():
    n = np.random.standard_normal
    s = mx_kscale(K)[:, None]
    u = mx_kscale(S)
    packed_xT = pack_weight(n((K, T)) * s)
    packed_w1 = pack_weight(n((S, N)) / np.sqrt(S) / u[:, None])
    return {
        "x_words": packed_xT[0],
        "x_scales": packed_xT[1],
        "wa": (n((K, H)) / np.sqrt(K) / s).astype(np.float32),
        "wb": (n((K, H)) / np.sqrt(K) / s).astype(np.float32),
        "gt": (np.random.uniform(0.5, 1.5, (S, 1)) * u[:, None]).astype(np.float32),
        "w1_words": packed_w1[0],
        "w1_scales": packed_w1[1],
        "offs": striped(np.random.permutation(T)[:S]),
        "two": striped(np.random.permutation(T)[:S]),
        "n1": striped8(np.stack([np.random.permutation(H) for _ in range(8)])),
        "n2": striped8(np.stack([np.random.permutation(H) for _ in range(8)])),
        "n3": striped8(np.stack([np.random.permutation(H) for _ in range(8)])),
        "n4": striped8(np.stack([np.random.permutation(H) for _ in range(8)])),
    }


def reference(x_words, x_scales, wa, wb, gt, w1_words, w1_scales, offs, two, n1, n2, n3, n4):
    xq = unpack_weight(x_words, x_scales)[:, unstriped(offs)]
    y = xq.T @ mxq(f64(wa), 0, "e4m3")
    x_two = unpack_weight(x_words, x_scales)[:, unstriped(two)]
    d = x_two.T @ mxq(f64(wb), 0, "e4m3")
    z = f64(gt) * (np.maximum(np.minimum(y - (0.5 * (y[np.arange(S)[:, None], runs(n1, S)])), d[np.arange(S)[:, None], runs(n2, S)]), d[np.arange(S)[:, None], runs(n3, S)]))
    h = unpack_weight(w1_words, w1_scales).T @ mxq(z, 0, "e4m3")
    rl = relu(h)
    ds = np.zeros((N, H))
    ds[np.arange(N)[:, None], runs(n4, N)] = rl
    out_0 = ds - (0.5 * h)
    return (out_0,) + planes(out_0)

@@ -1,0 +1,257 @@
+from contextlib import ExitStack
+
+import concourse.mybir as mybir
+
+K, T, S, N, H = 512, 2048, 512, 512, 512
+FLOPS = 2 * K * S * H * 2 + 2 * S * N * H
+
+F32 = mybir.dt.float32
+BF16 = mybir.dt.bfloat16
+I32 = mybir.dt.int32
+U32 = mybir.dt.uint32
+U16 = mybir.dt.uint16
+U8 = mybir.dt.uint8
+FP8X4 = mybir.dt.float8_e4m3fn_x4
+ALU = mybir.AluOpType
+ACT = mybir.ActivationFunctionType
+
+P = 128
+PACK = 4
+HALF = H // 2
+LIST_COLS = HALF // 16
+
+
+def tile_picked_twtclampbsend_none_po_kernel(
+    tc, x_words, x_scales, wa, wb, gt, w1_words, w1_scales, offs, two, n1, n2, n3, n4, out_0, out_1, out_2
+):
+    nc = tc.nc
+    with ExitStack() as ctx:
+        keep = ctx.enter_context(tc.tile_pool(name="keep", bufs=1))
+        stage = ctx.enter_context(tc.tile_pool(name="stage", bufs=2))
+        psum_yd = ctx.enter_context(tc.psum_pool(name="psum_yd", bufs=4))
+        psum_h = ctx.enter_context(tc.psum_pool(name="psum_h", bufs=1))
+
+        def held(shape, dtype, name):
+            return keep.tile(shape, dtype, name=name, align_bytes=64)
+
+        def load_list(source, name):
+            tile = held([P, S // 16], U16, name)
+            nc.sync.dma_start(tile[:], source)
+            return tile
+
+        def load_scale_rows(queue, tile, source):
+            for q in range(4):
+                queue.dma_start(tile[32 * q : 32 * q + 4, :].bitcast(I32), source[0, 4 * q : 4 * q + 4, :].bitcast(I32))
+
+        def words_of(source):
+            return source[0].rearrange("p n r -> p (n r)").bitcast(I32)
+
+        def half_of(lists, h):
+            return lists[:, h * LIST_COLS : (h + 1) * LIST_COLS]
+
+        xs = held([P, T], U8, "xs")
+        nc.vector.memset(xs[:].bitcast(I32), 0)
+        w1s_raw = held([P, N], U8, "w1s_raw")
+        nc.gpsimd.memset(w1s_raw[:].bitcast(I32), 0)
+
+        offs_t = load_list(offs, "offs_t")
+        two_t = load_list(two, "two_t")
+        n1_t = load_list(n1, "n1_t")
+        n2_t = load_list(n2, "n2_t")
+        n3_t = load_list(n3, "n3_t")
+        n4_t = load_list(n4, "n4_t")
+        gt_t = held([P, PACK], F32, "gt_t")
+        nc.sync.dma_start(gt_t[:], gt.rearrange("(p t) o -> p (t o)", t=PACK))
+        xw = held([P, T], I32, "xw")
+        nc.sync.dma_start(xw[:], words_of(x_words))
+        load_scale_rows(nc.scalar, xs, x_scales)
+
+        def load_weight_half(w, h):
+            raw = stage.tile([P, PACK, HALF], F32, name="w_raw")
+            nc.sync.dma_start(raw[:], w.rearrange("(p j) c -> p j c", j=PACK)[:, :, h * HALF : (h + 1) * HALF])
+            return raw
+
+        wa_raw = [load_weight_half(wa, h) for h in range(2)]
+
+        gt_abs = held([P, PACK], F32, "gt_abs")
+        gt_sign = held([P, PACK], F32, "gt_sign")
+        nc.scalar.activation(gt_abs[:], gt_t[:], ACT.Abs)
+        nc.scalar.activation(gt_sign[:], gt_t[:], ACT.Sign)
+
+        def interleave(copy, out, in_):
+            copy(out.rearrange("p (c i) j -> p c j i", i=4), in_.rearrange("p j (c i) -> p c j i", i=4))
+
+        def quantize(codes, scales, grouped):
+            nc.vector.quantize_mx(out=codes.bitcast(FP8X4), scales=scales, in_=grouped.rearrange("p c j -> p (c j)"))
+
+        def pick_scales(lists, name):
+            picked = held([P, S], U8, name + "_picked")
+            nc.vector.tensor_copy(picked[:], xs[:].indirect(lists[:]))
+            return picked
+
+        def deal(dealt, source):
+            nc.vector.tensor_copy(dealt[:].rearrange("p t m -> p m t"), source.rearrange("p (m t) -> p m t", t=PACK))
+
+        def pick_words(lists, name):
+            dealt = held([P, PACK, P], U32, name)
+            nc.vector.tensor_copy(dealt[:].rearrange("p t m -> p m t"), xw[:].bitcast(U32).indirect(lists[:]))
+            return dealt
+
+        def round_weight(raw, name):
+            grouped = held([P, H, PACK], BF16, name)
+            for h in range(2):
+                interleave(nc.scalar.copy, grouped[:, h * HALF : (h + 1) * HALF, :], raw[h][:])
+            return grouped
+
+        def project(x_codes, x_plane, w_codes, w_plane, name):
+            windows = []
+            for t in range(PACK):
+                bank = psum_yd.tile([P, H], F32, name="bank")
+                nc.tensor.matmul_mx(
+                    bank[:], lhsT=x_codes[:, t, :].bitcast(FP8X4), lhsT_scale=x_plane[:, t, :],
+                    rhs=w_codes[:].bitcast(FP8X4), rhs_scale=w_plane[:], start=True, stop=True,
+                )
+                window = held([P, H], F32, "%s%d" % (name, t))
+                nc.scalar.activation(window[:], bank[:], ACT.Copy, scale=gt_abs[:, t : t + 1])
+                windows.append(window)
+            return windows
+
+        xa_words = pick_words(offs_t, "xa_words")
+        xa_picked = pick_scales(offs_t, "xa")
+        xb_words = pick_words(two_t, "xb_words")
+        xa_plane = held([P, PACK, P], U8, "xa_plane")
+        deal(xa_plane, xa_picked[:])
+        wa_grouped = round_weight(wa_raw, "wa_grouped")
+        wa_codes = held([P, H], U32, "wa_codes")
+        wa_plane = held([P, H], U8, "wa_plane")
+        quantize(wa_codes[:], wa_plane[:], wa_grouped[:])
+        xb_picked = pick_scales(two_t, "xb")
+        y = project(xa_words, xa_plane, wa_codes, wa_plane, "y")
+        xb_plane = held([P, PACK, P], U8, "xb_plane")
+        deal(xb_plane, xb_picked[:])
+
+        wb_raw = [load_weight_half(wb, h) for h in range(2)]
+        w1w_raw = held([P, N], I32, "w1w_raw")
+        nc.sync.dma_start(w1w_raw[:], words_of(w1_words))
+        load_scale_rows(nc.sync, w1s_raw, w1_scales)
+        wb_grouped = round_weight(wb_raw, "wb_grouped")
+
+        w1_codes = held([P, PACK, P], U32, "w1_codes")
+        w1_plane = held([P, PACK, P], U8, "w1_plane")
+        deal(w1_codes, w1w_raw[:].bitcast(U32))
+        deal(w1_plane, w1s_raw[:])
+
+        first = held([P, 2, PACK, HALF], BF16, "first")
+        y_picked = [held([P, H], F32, "y_picked%d" % t) for t in range(PACK)]
+
+        def pick_y(t):
+            for h in range(2):
+                nc.vector.tensor_copy(y_picked[t][:, h * HALF : (h + 1) * HALF], y[t][:].indirect(half_of(n1_t, h)))
+
+        def subtract_half(t):
+            nc.vector.scalar_tensor_tensor(
+                first[:, :, t, :], y_picked[t][:].rearrange("p (h c) -> p h c", h=2), -0.5,
+                y[t][:].rearrange("p (h c) -> p h c", h=2), ALU.mult, ALU.add,
+            )
+
+        wb_codes = held([P, H], U32, "wb_codes")
+        wb_plane = held([P, H], U8, "wb_plane")
+        pick_y(0)
+        pick_y(1)
+        subtract_half(0)
+        quantize(wb_codes[:], wb_plane[:], wb_grouped[:])
+        d = project(xb_words, xb_plane, wb_codes, wb_plane, "d")
+        pick_y(2)
+        subtract_half(1)
+        pick_y(3)
+        subtract_half(2)
+
+        second = held([P, 2, PACK, HALF], BF16, "second")
+        third = held([P, 2, PACK, HALF], BF16, "third")
+        lesser = held([P, 2, PACK, HALF], BF16, "lesser")
+        chosen = held([P, 2, PACK, HALF], BF16, "chosen")
+        signed = held([P, 2, PACK, HALF], BF16, "signed")
+        z_grouped = held([P, H, PACK], BF16, "z_grouped")
+        z_codes = held([P, H], U32, "z_codes")
+        z_plane = held([P, H], U8, "z_plane")
+        h_banks = [psum_h.tile([P, H], F32, name="h_bank%d" % t) for t in range(PACK)]
+        positive = [held([P, H], F32, "positive%d" % t) for t in range(PACK)]
+        sent = [held([P, H], F32, "sent%d" % t) for t in range(PACK)]
+        result = held([P, PACK, H], F32, "result")
+
+        def cols(h):
+            return slice(h * HALF, (h + 1) * HALF)
+
+        def pick_d(picked, lists, h, t):
+            nc.vector.tensor_copy(picked[:, h, t, :], d[t][:].indirect(half_of(lists, h)))
+
+        def flat(tile, h):
+            return tile[:, h, :, :].rearrange("p t c -> p (t c)")
+
+        def take_min(h):
+            nc.vector.tensor_tensor(flat(lesser, h), flat(first, h), flat(second, h), ALU.min)
+
+        def take_max(h):
+            nc.vector.tensor_tensor(flat(chosen, h), flat(lesser, h), flat(third, h), ALU.max)
+            for t in range(PACK):
+                nc.scalar.activation(signed[:, h, t, :], chosen[:, h, t, :], ACT.Copy, scale=gt_sign[:, t : t + 1])
+            interleave(nc.scalar.copy, z_grouped[:, cols(h), :], signed[:, h, :, :])
+
+        def mix(h):
+            quantize(z_codes[:, cols(h)], z_plane[:, cols(h)], z_grouped[:, cols(h), :])
+            for t in range(PACK):
+                nc.tensor.matmul_mx(
+                    h_banks[t][:, cols(h)], lhsT=w1_codes[:, t, :].bitcast(FP8X4), lhsT_scale=w1_plane[:, t, :],
+                    rhs=z_codes[:, cols(h)].bitcast(FP8X4), rhs_scale=z_plane[:, cols(h)], start=True, stop=True,
+                )
+                nc.scalar.activation(positive[t][:, cols(h)], h_banks[t][:, cols(h)], ACT.Relu)
+
+        def send(h, t):
+            nc.vector.tensor_copy(sent[t][:].indirect(half_of(n4_t, h)), positive[t][:, cols(h)])
+
+        out_rows = out_0.rearrange("(p t) c -> p t c", t=PACK)
+
+        def finish(t):
+            nc.vector.scalar_tensor_tensor(result[:, t, :], h_banks[t][:], -0.5, sent[t][:], ALU.mult, ALU.add)
+            nc.sync.dma_start(out_rows[:, t, :], result[:, t, :])
+
+        pick_d(second, n2_t, 0, 0)
+        subtract_half(3)
+        for t in range(1, PACK):
+            pick_d(second, n2_t, 0, t)
+        for t in range(PACK - 1):
+            pick_d(third, n3_t, 0, t)
+        take_min(0)
+        pick_d(third, n3_t, 0, PACK - 1)
+        pick_d(second, n2_t, 1, 0)
+        take_max(0)
+        for t in range(1, PACK):
+            pick_d(second, n2_t, 1, t)
+        for t in range(PACK - 1):
+            pick_d(third, n3_t, 1, t)
+        mix(0)
+        take_min(1)
+        pick_d(third, n3_t, 1, PACK - 1)
+        send(0, 0)
+        take_max(1)
+        send(0, 1)
+        send(0, 2)
+        mix(1)
+        send(0, 3)
+        send(1, 0)
+        for t in range(1, PACK):
+            send(1, t)
+            finish(t - 1)
+        finish(PACK - 1)
+
+        out_grouped = held([P, H, PACK], BF16, "out_grouped")
+        out_codes = held([P, H], U32, "out_codes")
+        out_plane = held([P, H], U8, "out_plane")
+        interleave(nc.scalar.copy, out_grouped[:, cols(0), :], result[:, :, cols(0)])
+        interleave(nc.vector.tensor_copy, out_grouped[:, cols(1), :], result[:, :, cols(1)])
+        for h in (1, 0):
+            quantize(out_codes[:, cols(h)], out_plane[:, cols(h)], out_grouped[:, cols(h), :])
+            nc.sync.dma_start(words_of(out_1)[:, cols(h)], out_codes[:, cols(h)].bitcast(I32))
+        for q in range(4):
+            queue = nc.scalar if q % 2 else nc.sync
+            queue.dma_start(out_2[0, 4 * q : 4 * q + 4, :].bitcast(I32), out_plane[32 * q : 32 * q + 4, :].bitcast(I32))

@@ -1,6 +1,7 @@
 from contextlib import ExitStack
 
 import concourse.mybir as mybir
+from concourse.masks import make_identity
 
 K, T, S, N, H = 512, 2048, 512, 512, 512
 FLOPS = 2 * K * S * H * 2 + 2 * S * N * H
@@ -19,6 +20,7 @@ P = 128
 PACK = 4
 HALF = H // 2
 LIST_COLS = HALF // 16
+PAIRS = (slice(0, 2), slice(2, 4))
 
 
 def tile_picked_twtclampbsend_none_po_kernel(
@@ -27,12 +29,17 @@ def tile_picked_twtclampbsend_none_po_kernel(
     nc = tc.nc
     with ExitStack() as ctx:
         keep = ctx.enter_context(tc.tile_pool(name="keep", bufs=1))
-        stage = ctx.enter_context(tc.tile_pool(name="stage", bufs=2))
-        psum_yd = ctx.enter_context(tc.psum_pool(name="psum_yd", bufs=4))
-        psum_h = ctx.enter_context(tc.psum_pool(name="psum_h", bufs=1))
+        shared = ctx.enter_context(tc.tile_pool(name="shared", bufs=1))
+        psum = ctx.enter_context(tc.psum_pool(name="psum", bufs=1))
 
-        def held(shape, dtype, name):
-            return keep.tile(shape, dtype, name=name, align_bytes=64)
+        def held(shape, dtype, name, tag=None):
+            return keep.tile(shape, dtype, name=name, tag=tag or name, align_bytes=64)
+
+        def overlaid(shape, dtype, name, offset):
+            return shared.tile(shape, dtype, name=name, offset=offset, align_bytes=64)
+
+        def bank(number, shape, dtype, name):
+            return psum.tile(shape, dtype, name=name, tag="bank%d" % number)
 
         def load_list(source, name):
             tile = held([P, S // 16], U16, name)
@@ -49,29 +56,38 @@ def tile_picked_twtclampbsend_none_po_kernel(
         def half_of(lists, h):
             return lists[:, h * LIST_COLS : (h + 1) * LIST_COLS]
 
-        xs = held([P, T], U8, "xs")
-        nc.vector.memset(xs[:].bitcast(I32), 0)
-        w1s_raw = held([P, N], U8, "w1s_raw")
-        nc.gpsimd.memset(w1s_raw[:].bitcast(I32), 0)
+        def cols(h):
+            return slice(h * HALF, (h + 1) * HALF)
 
-        offs_t = load_list(offs, "offs_t")
-        two_t = load_list(two, "two_t")
-        n1_t = load_list(n1, "n1_t")
-        n2_t = load_list(n2, "n2_t")
-        n3_t = load_list(n3, "n3_t")
-        n4_t = load_list(n4, "n4_t")
-        gt_t = held([P, PACK], F32, "gt_t")
-        nc.sync.dma_start(gt_t[:], gt.rearrange("(p t) o -> p (t o)", t=PACK))
-        xw = held([P, T], I32, "xw")
-        nc.sync.dma_start(xw[:], words_of(x_words))
-        load_scale_rows(nc.scalar, xs, x_scales)
+        def block(c):
+            return slice(c * P, (c + 1) * P)
 
-        def load_weight_half(w, h):
-            raw = stage.tile([P, PACK, HALF], F32, name="w_raw")
-            nc.sync.dma_start(raw[:], w.rearrange("(p j) c -> p j c", j=PACK)[:, :, h * HALF : (h + 1) * HALF])
+        def flat(view):
+            return view.rearrange("p t c -> p (t c)")
+
+        def load_weight_half(w, h, name):
+            raw = held([P, PACK, HALF], F32, "%s_raw%d" % (name, h))
+            nc.sync.dma_start(raw[:], w.rearrange("(p j) c -> p j c", j=PACK)[:, :, cols(h)])
             return raw
 
-        wa_raw = [load_weight_half(wa, h) for h in range(2)]
+        xs = held([P, T], U8, "xs")
+        nc.gpsimd.memset(xs[:].bitcast(I32), 0)
+        w1s_raw = held([P, N], U8, "w1s_raw")
+        nc.vector.memset(w1s_raw[:].bitcast(I32), 0)
+        ident32 = held([P, P], F32, "ident32")
+        ident16 = held([P, P], BF16, "ident16")
+        make_identity(nc, ident32[:])
+        make_identity(nc, ident16[:])
+
+        load_scale_rows(nc.sync, xs, x_scales)
+        offs_t = load_list(offs, "offs_t")
+        xw = held([P, T], I32, "xw")
+        nc.sync.dma_start(xw[:], words_of(x_words))
+        two_t = load_list(two, "two_t")
+        wa_raw = [load_weight_half(wa, h, "wa") for h in range(2)]
+        gt_t = held([P, PACK], F32, "gt_t")
+        nc.sync.dma_start(gt_t[:], gt.rearrange("(p t) o -> p (t o)", t=PACK))
+        n1_t = load_list(n1, "n1_t")
 
         gt_abs = held([P, PACK], F32, "gt_abs")
         gt_sign = held([P, PACK], F32, "gt_sign")
@@ -82,7 +98,7 @@ def tile_picked_twtclampbsend_none_po_kernel(
             copy(out.rearrange("p (c i) j -> p c j i", i=4), in_.rearrange("p j (c i) -> p c j i", i=4))
 
         def quantize(codes, scales, grouped):
-            nc.vector.quantize_mx(out=codes.bitcast(FP8X4), scales=scales, in_=grouped.rearrange("p c j -> p (c j)"))
+            nc.vector.quantize_mx(out=codes.bitcast(FP8X4), scales=scales, in_=flat(grouped))
 
         def pick_scales(lists, name):
             picked = held([P, S], U8, name + "_picked")
@@ -92,164 +108,209 @@ def tile_picked_twtclampbsend_none_po_kernel(
         def deal(dealt, source):
             nc.vector.tensor_copy(dealt[:].rearrange("p t m -> p m t"), source.rearrange("p (m t) -> p m t", t=PACK))
 
-        def pick_words(lists, name):
-            dealt = held([P, PACK, P], U32, name)
+        def pick_words(lists, name, tag=None):
+            dealt = held([P, PACK, P], U32, name, tag)
             nc.vector.tensor_copy(dealt[:].rearrange("p t m -> p m t"), xw[:].bitcast(U32).indirect(lists[:]))
             return dealt
 
-        def round_weight(raw, name):
-            grouped = held([P, H, PACK], BF16, name)
+        def round_weight(raw, grouped):
             for h in range(2):
-                interleave(nc.scalar.copy, grouped[:, h * HALF : (h + 1) * HALF, :], raw[h][:])
+                interleave(nc.scalar.copy, grouped[:, cols(h), :], raw[h][:])
             return grouped
 
         def project(x_codes, x_plane, w_codes, w_plane, name):
             windows = []
             for t in range(PACK):
-                bank = psum_yd.tile([P, H], F32, name="bank")
+                acc = bank(t, [P, H], F32, "%s_acc%d" % (name, t))
                 nc.tensor.matmul_mx(
-                    bank[:], lhsT=x_codes[:, t, :].bitcast(FP8X4), lhsT_scale=x_plane[:, t, :],
+                    acc[:], lhsT=x_codes[:, t, :].bitcast(FP8X4), lhsT_scale=x_plane[:, t, :],
                     rhs=w_codes[:].bitcast(FP8X4), rhs_scale=w_plane[:], start=True, stop=True,
                 )
                 window = held([P, H], F32, "%s%d" % (name, t))
-                nc.scalar.activation(window[:], bank[:], ACT.Copy, scale=gt_abs[:, t : t + 1])
+                nc.scalar.activation(window[:], acc[:], ACT.Copy, scale=gt_abs[:, t : t + 1])
                 windows.append(window)
             return windows
 
-        xa_words = pick_words(offs_t, "xa_words")
+        def turned_sum(out, a, b):
+            nc.tensor.matmul(out, a, ident32[:], is_transpose=True, start=True, stop=False)
+            nc.tensor.matmul(out, b, ident32[:], is_transpose=True, start=False, stop=True)
+
         xa_picked = pick_scales(offs_t, "xa")
-        xb_words = pick_words(two_t, "xb_words")
+        xb_picked = pick_scales(two_t, "xb")
         xa_plane = held([P, PACK, P], U8, "xa_plane")
         deal(xa_plane, xa_picked[:])
-        wa_grouped = round_weight(wa_raw, "wa_grouped")
+        xa_words = pick_words(offs_t, "xa_words")
+        wa_grouped = round_weight(wa_raw, held([P, H, PACK], BF16, "wa_grouped"))
         wa_codes = held([P, H], U32, "wa_codes")
         wa_plane = held([P, H], U8, "wa_plane")
         quantize(wa_codes[:], wa_plane[:], wa_grouped[:])
-        xb_picked = pick_scales(two_t, "xb")
         y = project(xa_words, xa_plane, wa_codes, wa_plane, "y")
         xb_plane = held([P, PACK, P], U8, "xb_plane")
         deal(xb_plane, xb_picked[:])
+        xb_words = pick_words(two_t, "xb_words", tag="wa_grouped")
 
-        wb_raw = [load_weight_half(wb, h) for h in range(2)]
+        wb_raw = [load_weight_half(wb, h, "wb") for h in range(2)]
+        n2_t = load_list(n2, "n2_t")
+        n3_t = load_list(n3, "n3_t")
         w1w_raw = held([P, N], I32, "w1w_raw")
         nc.sync.dma_start(w1w_raw[:], words_of(w1_words))
         load_scale_rows(nc.sync, w1s_raw, w1_scales)
-        wb_grouped = round_weight(wb_raw, "wb_grouped")
+        n4_t = load_list(n4, "n4_t")
+        wb_grouped = round_weight(wb_raw, overlaid([P, H, PACK], BF16, "wb_grouped", 0))
 
-        w1_codes = held([P, PACK, P], U32, "w1_codes")
-        w1_plane = held([P, PACK, P], U8, "w1_plane")
-        deal(w1_codes, w1w_raw[:].bitcast(U32))
-        deal(w1_plane, w1s_raw[:])
+        y_picked = {}
 
-        first = held([P, 2, PACK, HALF], BF16, "first")
-        y_picked = [held([P, H], F32, "y_picked%d" % t) for t in range(PACK)]
+        def pick_y(h, t, tile=None):
+            y_picked[h, t] = held([P, HALF], F32, "y_picked%d%d" % (h, t)) if tile is None else tile
+            nc.vector.tensor_scalar(y_picked[h, t][:], y[t][:].indirect(half_of(n1_t, h)), -0.5, 0.0, ALU.mult, ALU.add)
 
-        def pick_y(t):
-            for h in range(2):
-                nc.vector.tensor_copy(y_picked[t][:, h * HALF : (h + 1) * HALF], y[t][:].indirect(half_of(n1_t, h)))
+        first = {}
 
-        def subtract_half(t):
-            nc.vector.scalar_tensor_tensor(
-                first[:, :, t, :], y_picked[t][:].rearrange("p (h c) -> p h c", h=2), -0.5,
-                y[t][:].rearrange("p (h c) -> p h c", h=2), ALU.mult, ALU.add,
-            )
+        def make_first(h, turn_banks, tag):
+            turned = held([P, PACK, HALF], BF16, "first_turned%d" % h, tag)
+            first[h] = bank(6 + h, [P, PACK, HALF], BF16, "first%d" % h)
+            for pair in range(2):
+                acc = bank(turn_banks[pair], [P, 2, HALF], F32, "first_acc%d%d" % (h, pair))
+                for u in range(2):
+                    t = 2 * pair + u
+                    for c in range(2):
+                        turned_sum(acc[:, u, block(c)], y[t][:, cols(h)][:, block(c)], y_picked[h, t][:, block(c)])
+                nc.scalar.copy(flat(turned[:, 2 * pair : 2 * pair + 2, :]), flat(acc[:]))
+            for t in range(PACK):
+                for c in range(2):
+                    nc.tensor.transpose(first[h][:, t, block(c)], turned[:, t, block(c)], ident16[:])
 
         wb_codes = held([P, H], U32, "wb_codes")
         wb_plane = held([P, H], U8, "wb_plane")
-        pick_y(0)
-        pick_y(1)
-        subtract_half(0)
+        for t in range(PACK):
+            pick_y(0, t)
+        for t in range(PACK - 1):
+            pick_y(1, t)
         quantize(wb_codes[:], wb_plane[:], wb_grouped[:])
         d = project(xb_words, xb_plane, wb_codes, wb_plane, "d")
-        pick_y(2)
-        subtract_half(1)
-        pick_y(3)
-        subtract_half(2)
+        pick_y(1, PACK - 1, overlaid([P, HALF], F32, "y_picked_last", 0))
+        make_first(0, (4, 5), "wb_raw1")
+        make_first(1, (2, 3), None)
 
-        second = held([P, 2, PACK, HALF], BF16, "second")
-        third = held([P, 2, PACK, HALF], BF16, "third")
-        lesser = held([P, 2, PACK, HALF], BF16, "lesser")
+        w1_codes = overlaid([P, PACK, P], U32, "w1_codes", 1024)
+        w1_plane = overlaid([P, PACK, P], U8, "w1_plane", 3072)
+        deal(w1_codes, w1w_raw[:].bitcast(U32))
+        deal(w1_plane, w1s_raw[:])
+
+        second = {}
+        third = {}
+        lesser = [held([P, PACK, HALF], BF16, "lesser%d" % h) for h in range(2)]
         chosen = held([P, 2, PACK, HALF], BF16, "chosen")
         signed = held([P, 2, PACK, HALF], BF16, "signed")
-        z_grouped = held([P, H, PACK], BF16, "z_grouped")
+        z_grouped = {}
         z_codes = held([P, H], U32, "z_codes")
         z_plane = held([P, H], U8, "z_plane")
-        h_banks = [psum_h.tile([P, H], F32, name="h_bank%d" % t) for t in range(PACK)]
-        positive = [held([P, H], F32, "positive%d" % t) for t in range(PACK)]
-        sent = [held([P, H], F32, "sent%d" % t) for t in range(PACK)]
+        h_banks = [bank(number, [P, H], F32, "h_acc%d" % t) for t, number in enumerate((0, 1, 4, 5))]
+        positive = {}
+        sent = {}
         result = held([P, PACK, H], F32, "result")
 
-        def cols(h):
-            return slice(h * HALF, (h + 1) * HALF)
-
         def pick_d(picked, lists, h, t):
-            nc.vector.tensor_copy(picked[:, h, t, :], d[t][:].indirect(half_of(lists, h)))
-
-        def flat(tile, h):
-            return tile[:, h, :, :].rearrange("p t c -> p (t c)")
+            nc.vector.tensor_copy(picked[:, t, :], d[t][:].indirect(half_of(lists, h)))
 
         def take_min(h):
-            nc.vector.tensor_tensor(flat(lesser, h), flat(first, h), flat(second, h), ALU.min)
+            for pair in PAIRS:
+                nc.vector.tensor_tensor(flat(lesser[h][:, pair]), flat(first[h][:, pair]), flat(second[h][:, pair]), ALU.min)
 
         def take_max(h):
-            nc.vector.tensor_tensor(flat(chosen, h), flat(lesser, h), flat(third, h), ALU.max)
+            for pair in PAIRS:
+                nc.vector.tensor_tensor(flat(chosen[:, h, pair]), flat(lesser[h][:, pair]), flat(third[h][:, pair]), ALU.max)
             for t in range(PACK):
                 nc.scalar.activation(signed[:, h, t, :], chosen[:, h, t, :], ACT.Copy, scale=gt_sign[:, t : t + 1])
-            interleave(nc.scalar.copy, z_grouped[:, cols(h), :], signed[:, h, :, :])
+            z_grouped[h] = held([P, HALF, PACK], BF16, "z_grouped%d" % h)
+            interleave(nc.scalar.copy, z_grouped[h][:], signed[:, h, :, :])
 
         def mix(h):
-            quantize(z_codes[:, cols(h)], z_plane[:, cols(h)], z_grouped[:, cols(h), :])
+            quantize(z_codes[:, cols(h)], z_plane[:, cols(h)], z_grouped[h][:])
             for t in range(PACK):
                 nc.tensor.matmul_mx(
                     h_banks[t][:, cols(h)], lhsT=w1_codes[:, t, :].bitcast(FP8X4), lhsT_scale=w1_plane[:, t, :],
                     rhs=z_codes[:, cols(h)].bitcast(FP8X4), rhs_scale=z_plane[:, cols(h)], start=True, stop=True,
                 )
-                nc.scalar.activation(positive[t][:, cols(h)], h_banks[t][:, cols(h)], ACT.Relu)
+                positive[h, t] = held([P, HALF], F32, "positive%d%d" % (h, t))
+                nc.scalar.activation(positive[h, t][:], h_banks[t][:, cols(h)], ACT.Relu)
 
-        def send(h, t):
-            nc.vector.tensor_copy(sent[t][:].indirect(half_of(n4_t, h)), positive[t][:, cols(h)])
+        def send(h, t, tag=None):
+            if h == 0:
+                sent[t] = held([P, H], F32, "sent%d" % t, tag)
+            nc.vector.tensor_copy(sent[t][:].indirect(half_of(n4_t, h)), positive[h, t][:])
 
         out_rows = out_0.rearrange("(p t) c -> p t c", t=PACK)
 
-        def finish(t):
+        def finish_on_vector(t):
             nc.vector.scalar_tensor_tensor(result[:, t, :], h_banks[t][:], -0.5, sent[t][:], ALU.mult, ALU.add)
             nc.sync.dma_start(out_rows[:, t, :], result[:, t, :])
 
-        pick_d(second, n2_t, 0, 0)
-        subtract_half(3)
-        for t in range(1, PACK):
-            pick_d(second, n2_t, 0, t)
-        for t in range(PACK - 1):
-            pick_d(third, n3_t, 0, t)
-        take_min(0)
-        pick_d(third, n3_t, 0, PACK - 1)
-        pick_d(second, n2_t, 1, 0)
-        take_max(0)
-        for t in range(1, PACK):
-            pick_d(second, n2_t, 1, t)
-        for t in range(PACK - 1):
-            pick_d(third, n3_t, 1, t)
-        mix(0)
-        take_min(1)
-        pick_d(third, n3_t, 1, PACK - 1)
-        send(0, 0)
-        take_max(1)
-        send(0, 1)
-        send(0, 2)
-        mix(1)
-        send(0, 3)
-        send(1, 0)
-        for t in range(1, PACK):
-            send(1, t)
-            finish(t - 1)
-        finish(PACK - 1)
+        minus_half = {}
 
+        def halve(t):
+            minus_half[t] = held([P, H], F32, "minus_half%d" % t)
+            nc.scalar.activation(minus_half[t][:], h_banks[t][:], ACT.Copy, scale=-0.5)
+
+        def finish_on_tensor(t):
+            acc = bank(2 + t % 2, [P, H], F32, "result_turned_acc%d" % t)
+            for c in range(H // P):
+                turned_sum(acc[:, block(c)], minus_half[t][:, block(c)], sent[t][:, block(c)])
+            turned = held([P, H], F32, "result_turned%d" % t)
+            nc.scalar.copy(turned[:], acc[:])
+            back = bank(6 + t % 2, [P, H], F32, "result_acc%d" % t)
+            for c in range(H // P):
+                nc.tensor.transpose(back[:, block(c)], turned[:, block(c)], ident32[:])
+            nc.scalar.copy(result[:, t, :], back[:])
+            nc.sync.dma_start(out_rows[:, t, :], result[:, t, :])
+
+        def finish_on_gpsimd(t):
+            nc.gpsimd.tensor_tensor(result[:, t, :], minus_half[t][:], sent[t][:], ALU.add)
+            nc.sync.dma_start(out_rows[:, t, :], result[:, t, :])
+
+        second[0] = held([P, PACK, HALF], BF16, "second0")
+        third[0] = held([P, PACK, HALF], BF16, "third0")
+        for t in range(PACK):
+            pick_d(second[0], n2_t, 0, t)
+        for t in range(PACK):
+            pick_d(third[0], n3_t, 0, t)
+        take_min(0)
+        take_max(0)
+        second[1] = held([P, PACK, HALF], BF16, "second1", tag="third0")
+        for t in range(PACK):
+            pick_d(second[1], n2_t, 1, t)
+        take_min(1)
+        mix(0)
+        third[1] = held([P, PACK, HALF], BF16, "third1", tag="z_grouped0")
+        for t in range(PACK):
+            pick_d(third[1], n3_t, 1, t)
+        take_max(1)
+        send(0, 0, tag="z_grouped0")
+        send(0, 1, tag="lesser1")
+        mix(1)
+        send(0, 2, tag="z_grouped1")
+        for t in range(PACK - 1):
+            halve(t)
         out_grouped = held([P, H, PACK], BF16, "out_grouped")
         out_codes = held([P, H], U32, "out_codes")
         out_plane = held([P, H], U8, "out_plane")
-        interleave(nc.scalar.copy, out_grouped[:, cols(0), :], result[:, :, cols(0)])
-        interleave(nc.vector.tensor_copy, out_grouped[:, cols(1), :], result[:, :, cols(1)])
-        for h in (1, 0):
+        for t in range(PACK - 1):
+            send(1, t)
+        finish_on_tensor(0)
+        finish_on_tensor(1)
+        interleave(nc.scalar.copy, out_grouped[:, :, 0:2], result[:, 0:2, :])
+        finish_on_gpsimd(2)
+        last = PACK - 1
+        send(0, last, tag="positive12")
+        send(1, last)
+        for h in range(2):
+            nc.vector.scalar_tensor_tensor(
+                result[:, last, cols(h)], h_banks[last][:, cols(h)], -0.5, sent[last][:, cols(h)], ALU.mult, ALU.add
+            )
+        nc.sync.dma_start(out_rows[:, last, :], result[:, last, :])
+        for h in range(2):
+            interleave(nc.vector.tensor_copy, out_grouped[:, cols(h), 2:4], result[:, 2:4, cols(h)])
+        for h in range(2):
             quantize(out_codes[:, cols(h)], out_plane[:, cols(h)], out_grouped[:, cols(h), :])
             nc.sync.dma_start(words_of(out_1)[:, cols(h)], out_codes[:, cols(h)].bitcast(I32))
         for q in range(4):

@@ -20,6 +20,7 @@ P = 128
 PACK = 4
 HALF = H // 2
 LIST_COLS = HALF // 16
+SCALAR_COLS = 192
 PAIRS = (slice(0, 2), slice(2, 4))
 
 
@@ -48,7 +49,7 @@ def tile_picked_twtclampbsend_none_po_kernel(
 
         def load_scale_rows(queue, tile, source):
             for q in range(4):
-                queue.dma_start(tile[32 * q : 32 * q + 4, :].bitcast(I32), source[0, 4 * q : 4 * q + 4, :].bitcast(I32))
+                queue.dma_start(tile[q:P:32, :].bitcast(I32), source[0, q:16:4, :].bitcast(I32))
 
         def words_of(source):
             return source[0].rearrange("p n r -> p (n r)").bitcast(I32)
@@ -79,7 +80,7 @@ def tile_picked_twtclampbsend_none_po_kernel(
         make_identity(nc, ident32[:])
         make_identity(nc, ident16[:])
 
-        load_scale_rows(nc.sync, xs, x_scales)
+        load_scale_rows(nc.scalar, xs, x_scales)
         offs_t = load_list(offs, "offs_t")
         xw = held([P, T], I32, "xw")
         nc.sync.dma_start(xw[:], words_of(x_words))
@@ -131,9 +132,11 @@ def tile_picked_twtclampbsend_none_po_kernel(
                 windows.append(window)
             return windows
 
-        def turned_sum(out, a, b):
-            nc.tensor.matmul(out, a, ident32[:], is_transpose=True, start=True, stop=False)
-            nc.tensor.matmul(out, b, ident32[:], is_transpose=True, start=False, stop=True)
+        def turned_sum(acc, early, late):
+            for c, part in enumerate(early):
+                nc.tensor.matmul(acc[:, block(c)], part, ident32[:], is_transpose=True, start=c == 0, stop=False)
+            for c, part in enumerate(late):
+                nc.tensor.matmul(acc[:, block(c)], part, ident32[:], is_transpose=True, start=False, stop=c == len(late) - 1)
 
         xa_picked = pick_scales(offs_t, "xa")
         xb_picked = pick_scales(two_t, "xb")
@@ -170,12 +173,14 @@ def tile_picked_twtclampbsend_none_po_kernel(
             turned = held([P, PACK, HALF], BF16, "first_turned%d" % h, tag)
             first[h] = bank(6 + h, [P, PACK, HALF], BF16, "first%d" % h)
             for pair in range(2):
-                acc = bank(turn_banks[pair], [P, 2, HALF], F32, "first_acc%d%d" % (h, pair))
-                for u in range(2):
-                    t = 2 * pair + u
-                    for c in range(2):
-                        turned_sum(acc[:, u, block(c)], y[t][:, cols(h)][:, block(c)], y_picked[h, t][:, block(c)])
-                nc.scalar.copy(flat(turned[:, 2 * pair : 2 * pair + 2, :]), flat(acc[:]))
+                acc = bank(turn_banks[pair], [P, 2 * HALF], F32, "first_acc%d%d" % (h, pair))
+                places = [(t, c) for t in (2 * pair, 2 * pair + 1) for c in range(2)]
+                turned_sum(
+                    acc,
+                    [y[t][:, cols(h)][:, block(c)] for t, c in places],
+                    [y_picked[h, t][:, block(c)] for t, c in places],
+                )
+                nc.scalar.copy(flat(turned[:, PAIRS[pair], :]), acc[:])
             for t in range(PACK):
                 for c in range(2):
                     nc.tensor.transpose(first[h][:, t, block(c)], turned[:, t, block(c)], ident16[:])
@@ -197,43 +202,57 @@ def tile_picked_twtclampbsend_none_po_kernel(
         deal(w1_codes, w1w_raw[:].bitcast(U32))
         deal(w1_plane, w1s_raw[:])
 
-        second = {}
-        third = {}
-        lesser = [held([P, PACK, HALF], BF16, "lesser%d" % h) for h in range(2)]
+        second, third, z_grouped, positive, sent = {}, {}, {}, {}, {}
+        lesser = held([P, 2, PACK, HALF], BF16, "lesser")
         chosen = held([P, 2, PACK, HALF], BF16, "chosen")
         signed = held([P, 2, PACK, HALF], BF16, "signed")
-        z_grouped = {}
         z_codes = held([P, H], U32, "z_codes")
         z_plane = held([P, H], U8, "z_plane")
         h_banks = [bank(number, [P, H], F32, "h_acc%d" % t) for t, number in enumerate((0, 1, 4, 5))]
-        positive = {}
-        sent = {}
         result = held([P, PACK, H], F32, "result")
+        last = PACK - 1
+        positive_last = held([P, H], F32, "positive_last")
 
-        def pick_d(picked, lists, h, t):
-            nc.vector.tensor_copy(picked[:, t, :], d[t][:].indirect(half_of(lists, h)))
+        def pick_d(picked, name, lists, h, tags):
+            for pair in range(2):
+                picked[h, pair] = held([P, 2, HALF], BF16, "%s%d%d" % (name, h, pair), tags[pair])
+                for u in range(2):
+                    nc.vector.tensor_copy(picked[h, pair][:, u, :], d[2 * pair + u][:].indirect(half_of(lists, h)))
 
         def take_min(h):
-            for pair in PAIRS:
-                nc.vector.tensor_tensor(flat(lesser[h][:, pair]), flat(first[h][:, pair]), flat(second[h][:, pair]), ALU.min)
+            for pair in range(2):
+                nc.vector.tensor_tensor(
+                    flat(lesser[:, h, PAIRS[pair]]), flat(first[h][:, PAIRS[pair]]), flat(second[h, pair][:]), ALU.min
+                )
 
         def take_max(h):
-            for pair in PAIRS:
-                nc.vector.tensor_tensor(flat(chosen[:, h, pair]), flat(lesser[h][:, pair]), flat(third[h][:, pair]), ALU.max)
+            for pair in range(2):
+                nc.vector.tensor_tensor(
+                    flat(chosen[:, h, PAIRS[pair]]), flat(lesser[:, h, PAIRS[pair]]), flat(third[h, pair][:]), ALU.max
+                )
             for t in range(PACK):
                 nc.scalar.activation(signed[:, h, t, :], chosen[:, h, t, :], ACT.Copy, scale=gt_sign[:, t : t + 1])
-            z_grouped[h] = held([P, HALF, PACK], BF16, "z_grouped%d" % h)
-            interleave(nc.scalar.copy, z_grouped[h][:], signed[:, h, :, :])
+
+        def quantize_z(h, pieces):
+            width = HALF // pieces
+            for piece in range(pieces):
+                grouped = held([P, width, PACK], BF16, "z_grouped%d%d" % (h, piece))
+                interleave(nc.scalar.copy, grouped[:], signed[:, h, :, piece * width : (piece + 1) * width])
+                span = slice(h * HALF + piece * width, h * HALF + (piece + 1) * width)
+                quantize(z_codes[:, span], z_plane[:, span], grouped[:])
 
         def mix(h):
-            quantize(z_codes[:, cols(h)], z_plane[:, cols(h)], z_grouped[h][:])
             for t in range(PACK):
                 nc.tensor.matmul_mx(
                     h_banks[t][:, cols(h)], lhsT=w1_codes[:, t, :].bitcast(FP8X4), lhsT_scale=w1_plane[:, t, :],
                     rhs=z_codes[:, cols(h)].bitcast(FP8X4), rhs_scale=z_plane[:, cols(h)], start=True, stop=True,
                 )
-                positive[h, t] = held([P, HALF], F32, "positive%d%d" % (h, t))
-                nc.scalar.activation(positive[h, t][:], h_banks[t][:, cols(h)], ACT.Relu)
+                if t == last:
+                    target = positive_last[:, cols(h)]
+                else:
+                    positive[h, t] = held([P, HALF], F32, "positive%d%d" % (h, t))
+                    target = positive[h, t][:]
+                nc.scalar.activation(target, h_banks[t][:, cols(h)], ACT.Relu)
 
         def send(h, t, tag=None):
             if h == 0:
@@ -241,11 +260,6 @@ def tile_picked_twtclampbsend_none_po_kernel(
             nc.vector.tensor_copy(sent[t][:].indirect(half_of(n4_t, h)), positive[h, t][:])
 
         out_rows = out_0.rearrange("(p t) c -> p t c", t=PACK)
-
-        def finish_on_vector(t):
-            nc.vector.scalar_tensor_tensor(result[:, t, :], h_banks[t][:], -0.5, sent[t][:], ALU.mult, ALU.add)
-            nc.sync.dma_start(out_rows[:, t, :], result[:, t, :])
-
         minus_half = {}
 
         def halve(t):
@@ -254,65 +268,55 @@ def tile_picked_twtclampbsend_none_po_kernel(
 
         def finish_on_tensor(t):
             acc = bank(2 + t % 2, [P, H], F32, "result_turned_acc%d" % t)
-            for c in range(H // P):
-                turned_sum(acc[:, block(c)], minus_half[t][:, block(c)], sent[t][:, block(c)])
+            blocks = [block(c) for c in range(H // P)]
+            turned_sum(acc, [minus_half[t][:, b] for b in blocks], [sent[t][:, b] for b in blocks])
             turned = held([P, H], F32, "result_turned%d" % t)
             nc.scalar.copy(turned[:], acc[:])
             back = bank(6 + t % 2, [P, H], F32, "result_acc%d" % t)
-            for c in range(H // P):
-                nc.tensor.transpose(back[:, block(c)], turned[:, block(c)], ident32[:])
+            for b in blocks:
+                nc.tensor.transpose(back[:, b], turned[:, b], ident32[:])
             nc.scalar.copy(result[:, t, :], back[:])
-            nc.sync.dma_start(out_rows[:, t, :], result[:, t, :])
+            nc.scalar.dma_start(out_rows[:, t, :], result[:, t, :])
 
-        def finish_on_gpsimd(t):
-            nc.gpsimd.tensor_tensor(result[:, t, :], minus_half[t][:], sent[t][:], ALU.add)
-            nc.sync.dma_start(out_rows[:, t, :], result[:, t, :])
-
-        second[0] = held([P, PACK, HALF], BF16, "second0")
-        third[0] = held([P, PACK, HALF], BF16, "third0")
-        for t in range(PACK):
-            pick_d(second[0], n2_t, 0, t)
-        for t in range(PACK):
-            pick_d(third[0], n3_t, 0, t)
+        pick_d(second, "second", n2_t, 0, (None, None))
+        pick_d(third, "third", n3_t, 0, (None, None))
         take_min(0)
         take_max(0)
-        second[1] = held([P, PACK, HALF], BF16, "second1", tag="third0")
-        for t in range(PACK):
-            pick_d(second[1], n2_t, 1, t)
+        pick_d(second, "second", n2_t, 1, ("third00", "third01"))
         take_min(1)
+        quantize_z(0, 2)
         mix(0)
-        third[1] = held([P, PACK, HALF], BF16, "third1", tag="z_grouped0")
-        for t in range(PACK):
-            pick_d(third[1], n3_t, 1, t)
+        pick_d(third, "third", n3_t, 1, ("z_grouped00", "z_grouped01"))
         take_max(1)
-        send(0, 0, tag="z_grouped0")
-        send(0, 1, tag="lesser1")
+        send(0, 0, tag="z_grouped00")
+        send(0, 1, tag="z_grouped01")
+        quantize_z(1, 1)
         mix(1)
-        send(0, 2, tag="z_grouped1")
-        for t in range(PACK - 1):
+        send(0, 2, tag="z_grouped10")
+        for t in range(last):
             halve(t)
+        for t in range(last):
+            send(1, t)
+        for t in range(last):
+            finish_on_tensor(t)
+        sent_last = held([P, 2 * H], F32, "sent_last", tag="positive12")
+        nc.vector.tensor_copy(sent_last[:].indirect(n4_t[:]), positive_last[:])
+
         out_grouped = held([P, H, PACK], BF16, "out_grouped")
         out_codes = held([P, H], U32, "out_codes")
         out_plane = held([P, H], U8, "out_plane")
-        for t in range(PACK - 1):
-            send(1, t)
-        finish_on_tensor(0)
-        finish_on_tensor(1)
-        interleave(nc.scalar.copy, out_grouped[:, :, 0:2], result[:, 0:2, :])
-        finish_on_gpsimd(2)
-        last = PACK - 1
-        send(0, last, tag="positive12")
-        send(1, last)
-        for h in range(2):
+        on_scalar, rest = slice(0, SCALAR_COLS), slice(SCALAR_COLS, H)
+        for span in (on_scalar, rest):
             nc.vector.scalar_tensor_tensor(
-                result[:, last, cols(h)], h_banks[last][:, cols(h)], -0.5, sent[last][:, cols(h)], ALU.mult, ALU.add
+                result[:, last, span], h_banks[last][:, span], -0.5, sent_last[:, span], ALU.mult, ALU.add
             )
         nc.sync.dma_start(out_rows[:, last, :], result[:, last, :])
-        for h in range(2):
-            interleave(nc.vector.tensor_copy, out_grouped[:, cols(h), 2:4], result[:, 2:4, cols(h)])
-        for h in range(2):
+        interleave(nc.scalar.copy, out_grouped[:, on_scalar, :], result[:, :, on_scalar])
+        for span in (cols(1), slice(SCALAR_COLS, HALF)):
+            interleave(nc.vector.tensor_copy, out_grouped[:, span, :], result[:, :, span])
+        for h in (1, 0):
             quantize(out_codes[:, cols(h)], out_plane[:, cols(h)], out_grouped[:, cols(h), :])
             nc.sync.dma_start(words_of(out_1)[:, cols(h)], out_codes[:, cols(h)].bitcast(I32))
         for q in range(4):
             queue = nc.scalar if q % 2 else nc.sync
-            queue.dma_start(out_2[0, 4 * q : 4 * q + 4, :].bitcast(I32), out_plane[32 * q : 32 * q + 4, :].bitcast(I32))
+            queue.dma_start(out_2[0, q:16:4, :].bitcast(I32), out_plane[q:P:32, :].bitcast(I32))

from contextlib import ExitStack

import concourse.mybir as mybir
from concourse.masks import make_identity

K, T, S, N, H = 512, 2048, 512, 512, 512
FLOPS = 2 * K * S * H * 2 + 2 * S * N * H

F32 = mybir.dt.float32
BF16 = mybir.dt.bfloat16
I32 = mybir.dt.int32
U32 = mybir.dt.uint32
U16 = mybir.dt.uint16
U8 = mybir.dt.uint8
FP8X4 = mybir.dt.float8_e4m3fn_x4
ALU = mybir.AluOpType
ACT = mybir.ActivationFunctionType

P = 128
PACK = 4
HALF = H // 2
LIST_COLS = HALF // 16
SCALAR_COLS = 192
PAIRS = (slice(0, 2), slice(2, 4))


def tile_picked_twtclampbsend_none_po_kernel(
    tc, x_words, x_scales, wa, wb, gt, w1_words, w1_scales, offs, two, n1, n2, n3, n4, out_0, out_1, out_2
):
    nc = tc.nc
    with ExitStack() as ctx:
        keep = ctx.enter_context(tc.tile_pool(name="keep", bufs=1))
        shared = ctx.enter_context(tc.tile_pool(name="shared", bufs=1))
        psum = ctx.enter_context(tc.psum_pool(name="psum", bufs=1))

        def held(shape, dtype, name, tag=None):
            return keep.tile(shape, dtype, name=name, tag=tag or name, align_bytes=64)

        def overlaid(shape, dtype, name, offset):
            return shared.tile(shape, dtype, name=name, offset=offset, align_bytes=64)

        def bank(number, shape, dtype, name):
            return psum.tile(shape, dtype, name=name, tag="bank%d" % number)

        def load_list(source, name):
            tile = held([P, S // 16], U16, name)
            nc.sync.dma_start(tile[:], source)
            return tile

        def load_scale_rows(queue, tile, source):
            for q in range(4):
                queue.dma_start(tile[q:P:32, :].bitcast(I32), source[0, q:16:4, :].bitcast(I32))

        def words_of(source):
            return source[0].rearrange("p n r -> p (n r)").bitcast(I32)

        def half_of(lists, h):
            return lists[:, h * LIST_COLS : (h + 1) * LIST_COLS]

        def cols(h):
            return slice(h * HALF, (h + 1) * HALF)

        def block(c):
            return slice(c * P, (c + 1) * P)

        def flat(view):
            return view.rearrange("p t c -> p (t c)")

        def load_weight_half(w, h, name):
            raw = held([P, PACK, HALF], F32, "%s_raw%d" % (name, h))
            nc.sync.dma_start(raw[:], w.rearrange("(p j) c -> p j c", j=PACK)[:, :, cols(h)])
            return raw

        xs = held([P, T], U8, "xs")
        nc.gpsimd.memset(xs[:].bitcast(I32), 0)
        w1s_raw = held([P, N], U8, "w1s_raw")
        nc.vector.memset(w1s_raw[:].bitcast(I32), 0)
        ident32 = held([P, P], F32, "ident32")
        ident16 = held([P, P], BF16, "ident16")
        make_identity(nc, ident32[:])
        make_identity(nc, ident16[:])

        load_scale_rows(nc.scalar, xs, x_scales)
        offs_t = load_list(offs, "offs_t")
        xw = held([P, T], I32, "xw")
        nc.sync.dma_start(xw[:], words_of(x_words))
        two_t = load_list(two, "two_t")
        wa_raw = [load_weight_half(wa, h, "wa") for h in range(2)]
        gt_t = held([P, PACK], F32, "gt_t")
        nc.sync.dma_start(gt_t[:], gt.rearrange("(p t) o -> p (t o)", t=PACK))
        n1_t = load_list(n1, "n1_t")

        gt_abs = held([P, PACK], F32, "gt_abs")
        gt_sign = held([P, PACK], F32, "gt_sign")
        nc.scalar.activation(gt_abs[:], gt_t[:], ACT.Abs)
        nc.scalar.activation(gt_sign[:], gt_t[:], ACT.Sign)

        def interleave(copy, out, in_):
            copy(out.rearrange("p (c i) j -> p c j i", i=4), in_.rearrange("p j (c i) -> p c j i", i=4))

        def quantize(codes, scales, grouped):
            nc.vector.quantize_mx(out=codes.bitcast(FP8X4), scales=scales, in_=flat(grouped))

        def pick_scales(lists, name):
            picked = held([P, S], U8, name + "_picked")
            nc.vector.tensor_copy(picked[:], xs[:].indirect(lists[:]))
            return picked

        def deal(dealt, source):
            nc.vector.tensor_copy(dealt[:].rearrange("p t m -> p m t"), source.rearrange("p (m t) -> p m t", t=PACK))

        def pick_words(lists, name, tag=None):
            dealt = held([P, PACK, P], U32, name, tag)
            nc.vector.tensor_copy(dealt[:].rearrange("p t m -> p m t"), xw[:].bitcast(U32).indirect(lists[:]))
            return dealt

        def round_weight(raw, grouped):
            for h in range(2):
                interleave(nc.scalar.copy, grouped[:, cols(h), :], raw[h][:])
            return grouped

        def project(x_codes, x_plane, w_codes, w_plane, name):
            windows = []
            for t in range(PACK):
                acc = bank(t, [P, H], F32, "%s_acc%d" % (name, t))
                nc.tensor.matmul_mx(
                    acc[:], lhsT=x_codes[:, t, :].bitcast(FP8X4), lhsT_scale=x_plane[:, t, :],
                    rhs=w_codes[:].bitcast(FP8X4), rhs_scale=w_plane[:], start=True, stop=True,
                )
                window = held([P, H], F32, "%s%d" % (name, t))
                nc.scalar.activation(window[:], acc[:], ACT.Copy, scale=gt_abs[:, t : t + 1])
                windows.append(window)
            return windows

        def turned_sum(acc, early, late):
            for c, part in enumerate(early):
                nc.tensor.matmul(acc[:, block(c)], part, ident32[:], is_transpose=True, start=c == 0, stop=False)
            for c, part in enumerate(late):
                nc.tensor.matmul(acc[:, block(c)], part, ident32[:], is_transpose=True, start=False, stop=c == len(late) - 1)

        xa_picked = pick_scales(offs_t, "xa")
        xb_picked = pick_scales(two_t, "xb")
        xa_plane = held([P, PACK, P], U8, "xa_plane")
        deal(xa_plane, xa_picked[:])
        xa_words = pick_words(offs_t, "xa_words")
        wa_grouped = round_weight(wa_raw, held([P, H, PACK], BF16, "wa_grouped"))
        wa_codes = held([P, H], U32, "wa_codes")
        wa_plane = held([P, H], U8, "wa_plane")
        quantize(wa_codes[:], wa_plane[:], wa_grouped[:])
        y = project(xa_words, xa_plane, wa_codes, wa_plane, "y")
        xb_plane = held([P, PACK, P], U8, "xb_plane")
        deal(xb_plane, xb_picked[:])
        xb_words = pick_words(two_t, "xb_words", tag="wa_grouped")

        wb_raw = [load_weight_half(wb, h, "wb") for h in range(2)]
        n2_t = load_list(n2, "n2_t")
        n3_t = load_list(n3, "n3_t")
        w1w_raw = held([P, N], I32, "w1w_raw")
        nc.sync.dma_start(w1w_raw[:], words_of(w1_words))
        load_scale_rows(nc.sync, w1s_raw, w1_scales)
        n4_t = load_list(n4, "n4_t")
        wb_grouped = round_weight(wb_raw, overlaid([P, H, PACK], BF16, "wb_grouped", 0))

        y_picked = {}

        def pick_y(h, t, tile=None):
            y_picked[h, t] = held([P, HALF], F32, "y_picked%d%d" % (h, t)) if tile is None else tile
            nc.vector.tensor_scalar(y_picked[h, t][:], y[t][:].indirect(half_of(n1_t, h)), -0.5, 0.0, ALU.mult, ALU.add)

        first = {}

        def make_first(h, turn_banks, tag):
            turned = held([P, PACK, HALF], BF16, "first_turned%d" % h, tag)
            first[h] = bank(6 + h, [P, PACK, HALF], BF16, "first%d" % h)
            for pair in range(2):
                acc = bank(turn_banks[pair], [P, 2 * HALF], F32, "first_acc%d%d" % (h, pair))
                places = [(t, c) for t in (2 * pair, 2 * pair + 1) for c in range(2)]
                turned_sum(
                    acc,
                    [y[t][:, cols(h)][:, block(c)] for t, c in places],
                    [y_picked[h, t][:, block(c)] for t, c in places],
                )
                nc.scalar.copy(flat(turned[:, PAIRS[pair], :]), acc[:])
            for t in range(PACK):
                for c in range(2):
                    nc.tensor.transpose(first[h][:, t, block(c)], turned[:, t, block(c)], ident16[:])

        wb_codes = held([P, H], U32, "wb_codes")
        wb_plane = held([P, H], U8, "wb_plane")
        for t in range(PACK):
            pick_y(0, t)
        for t in range(PACK - 1):
            pick_y(1, t)
        quantize(wb_codes[:], wb_plane[:], wb_grouped[:])
        d = project(xb_words, xb_plane, wb_codes, wb_plane, "d")
        pick_y(1, PACK - 1, overlaid([P, HALF], F32, "y_picked_last", 0))
        make_first(0, (4, 5), "wb_raw1")
        make_first(1, (2, 3), None)

        w1_codes = overlaid([P, PACK, P], U32, "w1_codes", 1024)
        w1_plane = overlaid([P, PACK, P], U8, "w1_plane", 3072)
        deal(w1_codes, w1w_raw[:].bitcast(U32))
        deal(w1_plane, w1s_raw[:])

        second, third, z_grouped, positive, sent = {}, {}, {}, {}, {}
        lesser = held([P, 2, PACK, HALF], BF16, "lesser")
        chosen = held([P, 2, PACK, HALF], BF16, "chosen")
        signed = held([P, 2, PACK, HALF], BF16, "signed")
        z_codes = held([P, H], U32, "z_codes")
        z_plane = held([P, H], U8, "z_plane")
        h_banks = [bank(number, [P, H], F32, "h_acc%d" % t) for t, number in enumerate((0, 1, 4, 5))]
        result = held([P, PACK, H], F32, "result")
        last = PACK - 1
        positive_last = held([P, H], F32, "positive_last")

        def pick_d(picked, name, lists, h, tags):
            for pair in range(2):
                picked[h, pair] = held([P, 2, HALF], BF16, "%s%d%d" % (name, h, pair), tags[pair])
                for u in range(2):
                    nc.vector.tensor_copy(picked[h, pair][:, u, :], d[2 * pair + u][:].indirect(half_of(lists, h)))

        def take_min(h):
            for pair in range(2):
                nc.vector.tensor_tensor(
                    flat(lesser[:, h, PAIRS[pair]]), flat(first[h][:, PAIRS[pair]]), flat(second[h, pair][:]), ALU.min
                )

        def take_max(h):
            for pair in range(2):
                nc.vector.tensor_tensor(
                    flat(chosen[:, h, PAIRS[pair]]), flat(lesser[:, h, PAIRS[pair]]), flat(third[h, pair][:]), ALU.max
                )
            for t in range(PACK):
                nc.scalar.activation(signed[:, h, t, :], chosen[:, h, t, :], ACT.Copy, scale=gt_sign[:, t : t + 1])

        def quantize_z(h, pieces):
            width = HALF // pieces
            for piece in range(pieces):
                grouped = held([P, width, PACK], BF16, "z_grouped%d%d" % (h, piece))
                interleave(nc.scalar.copy, grouped[:], signed[:, h, :, piece * width : (piece + 1) * width])
                span = slice(h * HALF + piece * width, h * HALF + (piece + 1) * width)
                quantize(z_codes[:, span], z_plane[:, span], grouped[:])

        def mix(h):
            for t in range(PACK):
                nc.tensor.matmul_mx(
                    h_banks[t][:, cols(h)], lhsT=w1_codes[:, t, :].bitcast(FP8X4), lhsT_scale=w1_plane[:, t, :],
                    rhs=z_codes[:, cols(h)].bitcast(FP8X4), rhs_scale=z_plane[:, cols(h)], start=True, stop=True,
                )
                if t == last:
                    target = positive_last[:, cols(h)]
                else:
                    positive[h, t] = held([P, HALF], F32, "positive%d%d" % (h, t))
                    target = positive[h, t][:]
                nc.scalar.activation(target, h_banks[t][:, cols(h)], ACT.Relu)

        def send(h, t, tag=None):
            if h == 0:
                sent[t] = held([P, H], F32, "sent%d" % t, tag)
            nc.vector.tensor_copy(sent[t][:].indirect(half_of(n4_t, h)), positive[h, t][:])

        out_rows = out_0.rearrange("(p t) c -> p t c", t=PACK)
        minus_half = {}

        def halve(t):
            minus_half[t] = held([P, H], F32, "minus_half%d" % t)
            nc.scalar.activation(minus_half[t][:], h_banks[t][:], ACT.Copy, scale=-0.5)

        def finish_on_tensor(t):
            acc = bank(2 + t % 2, [P, H], F32, "result_turned_acc%d" % t)
            blocks = [block(c) for c in range(H // P)]
            turned_sum(acc, [minus_half[t][:, b] for b in blocks], [sent[t][:, b] for b in blocks])
            turned = held([P, H], F32, "result_turned%d" % t)
            nc.scalar.copy(turned[:], acc[:])
            back = bank(6 + t % 2, [P, H], F32, "result_acc%d" % t)
            for b in blocks:
                nc.tensor.transpose(back[:, b], turned[:, b], ident32[:])
            nc.scalar.copy(result[:, t, :], back[:])
            nc.scalar.dma_start(out_rows[:, t, :], result[:, t, :])

        pick_d(second, "second", n2_t, 0, (None, None))
        pick_d(third, "third", n3_t, 0, (None, None))
        take_min(0)
        take_max(0)
        pick_d(second, "second", n2_t, 1, ("third00", "third01"))
        take_min(1)
        quantize_z(0, 2)
        mix(0)
        pick_d(third, "third", n3_t, 1, ("z_grouped00", "z_grouped01"))
        take_max(1)
        send(0, 0, tag="z_grouped00")
        send(0, 1, tag="z_grouped01")
        quantize_z(1, 1)
        mix(1)
        send(0, 2, tag="z_grouped10")
        for t in range(last):
            halve(t)
        for t in range(last):
            send(1, t)
        for t in range(last):
            finish_on_tensor(t)
        sent_last = held([P, 2 * H], F32, "sent_last", tag="positive12")
        nc.vector.tensor_copy(sent_last[:].indirect(n4_t[:]), positive_last[:])

        out_grouped = held([P, H, PACK], BF16, "out_grouped")
        out_codes = held([P, H], U32, "out_codes")
        out_plane = held([P, H], U8, "out_plane")
        on_scalar, rest = slice(0, SCALAR_COLS), slice(SCALAR_COLS, H)
        for span in (on_scalar, rest):
            nc.vector.scalar_tensor_tensor(
                result[:, last, span], h_banks[last][:, span], -0.5, sent_last[:, span], ALU.mult, ALU.add
            )
        nc.sync.dma_start(out_rows[:, last, :], result[:, last, :])
        interleave(nc.scalar.copy, out_grouped[:, on_scalar, :], result[:, :, on_scalar])
        for span in (cols(1), slice(SCALAR_COLS, HALF)):
            interleave(nc.vector.tensor_copy, out_grouped[:, span, :], result[:, :, span])
        for h in (1, 0):
            quantize(out_codes[:, cols(h)], out_plane[:, cols(h)], out_grouped[:, cols(h), :])
            nc.sync.dma_start(words_of(out_1)[:, cols(h)], out_codes[:, cols(h)].bitcast(I32))
        for q in range(4):
            queue = nc.scalar if q % 2 else nc.sync
            queue.dma_start(out_2[0, q:16:4, :].bitcast(I32), out_plane[q:P:32, :].bitcast(I32))
